import numpy as np
import ml_dtypes


def mxq(x, axis, fmt="e4m3"):
    dtype, down = {"e4m3": (ml_dtypes.float8_e4m3fn, 7), "e5m2": (ml_dtypes.float8_e5m2, 14)}[fmt]
    v = np.moveaxis(np.asarray(x, np.float32).astype(ml_dtypes.bfloat16).astype(np.float64), axis, -1)
    blocks = v.reshape(v.shape[:-1] + (-1, 32))
    amax = np.abs(blocks).max(-1, keepdims=True)
    byte = np.maximum(np.where(amax > 0, np.frexp(amax)[1] - 1 + 127, 0) - down, 1)
    scale = np.exp2(byte - 127.0)
    codes = (blocks / scale).astype(np.float32).astype(dtype).astype(np.float64)
    return np.moveaxis((codes * scale).reshape(v.shape), -1, axis)


WIDE = False


def mx_kscale(k):
    if not WIDE:
        return np.ones(k)
    levels = np.array([10, -10, 5, -5, 0])
    if k % 512:
        return np.exp2(np.random.permutation(np.resize(levels, k // 32))).repeat(32)
    a = np.empty((k // 512, 16))
    for p in range(k // 512):
        a[p, :8] = np.random.permutation(np.resize(levels, 8))
        for g in range(8):
            far = levels[np.abs(levels - a[p, g]) >= 10]
            a[p, g + 8] = far[np.random.randint(len(far))]
    return np.exp2(a.ravel()).repeat(32)


BF16 = ml_dtypes.bfloat16


def bf(x):
    return np.asarray(x, np.float32).astype(BF16)


def f64(x):
    return np.asarray(x).astype(np.float64)


T, L, S = 1536, 1024, 512


def setup_inputs():
    s = mx_kscale(T)
    t = mx_kscale(L)
    u = mx_kscale(T)
    light = np.random.standard_normal((T, L))
    shade = 0.5 * np.random.standard_normal((T, T)) / np.sqrt(T)
    crown_gain = 1 + 0.1 * np.random.standard_normal(T)
    transfer = 0.35 * np.random.standard_normal((L, L)) / np.sqrt(L)
    layer_gain = 1 + 0.1 * np.random.standard_normal(L)
    compete = np.random.standard_normal((S, T)) / np.sqrt(T)
    return {"light": bf(light * s[:, None] * t),
            "shade": bf(shade * u[:, None] / s),
            "crown_gain": bf(crown_gain * u / s),
            "transfer": bf(transfer / t[:, None]),
            "layer_gain": bf(layer_gain / t),
            "compete": bf(compete / u),
            "bias": bf(0.3 * np.random.standard_normal(S))}


def reference(light, shade, crown_gain, transfer, layer_gain, compete, bias):
    x = f64(light)
    p1 = mxq(f64(shade), 1, "e4m3") @ mxq(x, 0, "e4m3")
    h1 = x * f64(crown_gain)[:, None] - np.maximum(p1, 0)
    p2 = mxq(h1, 1, "e4m3") @ mxq(f64(transfer), 0, "e4m3")
    h2 = h1 * f64(layer_gain) + p2
    p3 = mxq(f64(compete), 1, "e4m3") @ mxq(h2, 0, "e4m3")
    return p3 + f64(bias)[:, None]

@@ -1,0 +1,357 @@
+from contextlib import ExitStack
+
+import concourse.mybir as mybir
+from concourse.masks import make_identity
+
+T, L, S = 1536, 1024, 512
+
+FLOPS = 2 * (T * T * L + T * L * L + S * T * L)
+
+F32 = mybir.dt.float32
+BF16 = mybir.dt.bfloat16
+U32 = mybir.dt.uint32
+U8 = mybir.dt.uint8
+FP8X4 = mybir.dt.float8_e4m3fn_x4
+ALU = mybir.AluOpType
+ACT = mybir.ActivationFunctionType
+
+P = 128
+K = 512
+KT = T // K
+KL = L // K
+NT = T // P
+H = 512
+
+
+def tile_canopy_shading_competition_t1_kernel(
+    tc, light, shade, crown_gain, transfer, layer_gain, compete, bias, out
+):
+    nc = tc.nc
+    with ExitStack() as ctx:
+        keep = ctx.enter_context(tc.tile_pool(name="keep", bufs=1))
+        work = ctx.enter_context(tc.tile_pool(name="work", bufs=2))
+        psum = ctx.enter_context(tc.psum_pool(name="psum", bufs=1))
+        ctx.enter_context(tc.manual_schedule())
+
+        def load(name, shape, src):
+            t = keep.tile(shape, BF16, name=name, tag=name, align_bytes=64)
+            nc.sync.dma_start(out=t[:], in_=src)
+            return t
+
+        light_rows = [
+            light[K * g : K * (g + 1), :].rearrange("(p j) l -> p j l", j=4) for g in range(KT)
+        ]
+        cg_b = load("cg_b", [P, KT, 4], crown_gain.rearrange("(g p j) -> p g j", g=KT, j=4))
+        light_raw = []
+        shade_raw = []
+
+        def load_light(g):
+            t = keep.tile([P, 4, L], BF16, name="light%d" % g, tag="light%d" % g, align_bytes=64)
+            for h in range(2):
+                nc.sync.dma_start(
+                    out=t[:, :, H * h : H * (h + 1)], in_=light_rows[g][:, :, H * h : H * (h + 1)]
+                )
+            light_raw.append(t)
+
+        def load_shade(q):
+            g, a = q // 2, 2 * (q % 2)
+            src = shade[K * g : K * (g + 1), :].rearrange("(p j) k -> p j k", j=4)
+            t = work.tile([P, 2, T], BF16, name="rows", tag="rows", bufs=4, align_bytes=64)
+            nc.sync.dma_start(out=t[:], in_=src[:, a : a + 2, :])
+            shade_raw.append(t)
+
+        load_light(0)
+        load_light(1)
+        load_shade(0)
+        load_light(2)
+        load_shade(1)
+        transfer_raw = [
+            load("transfer%d" % g, [P, 4, L], transfer[K * g : K * (g + 1), :].rearrange("(p j) n -> p j n", j=4))
+            for g in range(KL)
+        ]
+        lg_b = load("lg_b", [P, L], layer_gain.partition_broadcast(P))
+        for q in range(2, 6):
+            load_shade(q)
+        compete_rows = compete.rearrange("(p m) k -> p m k", m=4)
+        for q in range(2):
+            t = work.tile([P, 2, T], BF16, name="rows", tag="rows", bufs=4, align_bytes=64)
+            nc.sync.dma_start(out=t[:], in_=compete_rows[:, 2 * q : 2 * q + 2, :])
+            shade_raw.append(t)
+        bias_b = load("bias_b", [P, 4], bias.rearrange("(p m) -> p m", m=4))
+
+        ident = keep.tile([P, P], F32, name="ident", tag="ident")
+        make_identity(nc, ident[:])
+        warm = keep.tile([P, 1], F32, name="warm", tag="warm")
+        nc.vector.memset(warm[:], 0.0)
+        nc.scalar.activation(out=warm[:], in_=warm[:], func=ACT.Copy)
+        cg = keep.tile([P, KT, 4], F32, name="cg", tag="cg")
+        nc.vector.tensor_copy(out=cg[:], in_=cg_b[:])
+
+        def operand(name, cols, bufs=1):
+            codes = keep.tile([P, cols], U32, name=name + "_c", tag=name + "_c", bufs=bufs, align_bytes=64)
+            scales = keep.tile([P, cols], U8, name=name + "_s", tag=name + "_s", bufs=bufs, align_bytes=64)
+            return codes, scales
+
+        def quantize(dst, lo, n, grouped):
+            nc.vector.quantize_mx(
+                out=dst[0][:, lo : lo + n].bitcast(FP8X4), scales=dst[1][:, lo : lo + n], in_=grouped
+            )
+
+        def mm(acc, st, so, mv, mo, n, start, stop):
+            nc.tensor.matmul_mx(
+                out=acc,
+                lhsT=st[0][:, so : so + P].bitcast(FP8X4),
+                lhsT_scale=st[1][:, so : so + P],
+                rhs=mv[0][:, mo : mo + n].bitcast(FP8X4),
+                rhs_scale=mv[1][:, mo : mo + n],
+                start=start,
+                stop=stop,
+            )
+
+        def copy(eng, dst, src):
+            if eng == "v":
+                nc.vector.tensor_copy(out=dst, in_=src)
+            else:
+                nc.scalar.copy(out=dst, in_=src)
+
+        def bank(tag):
+            return psum.tile([P, 512], F32, name=tag, tag=tag)
+
+        def interleave(eng, raw, h):
+            g = work.tile([P, H, 4], BF16, name="grouped", tag="grouped", bufs=3, align_bytes=64)
+            copy(
+                eng,
+                g[:].rearrange("p (c i) t -> p c t i", i=4),
+                raw[:, :, H * h : H * (h + 1)].rearrange("p t (c i) -> p c t i", i=4),
+            )
+            return g
+
+        light_q = [operand("lightq%d" % g, L) for g in range(KT)]
+        transfer_q = [operand("transferq%d" % g, L) for g in range(KL)]
+
+        pair_q = {}
+        pair_banks = {}
+        pair_grouped = {}
+
+        def turn_pair(q):
+            pair_banks[q] = []
+            for g in range(KT):
+                b = bank("st%d" % g)
+                v = b[:].rearrange("p (u a r) -> p u a r", u=2, a=2)
+                for a in range(2):
+                    words = shade_raw[q][:, a, :].bitcast(F32)
+                    for u in range(2):
+                        nc.tensor.transpose(
+                            v[:, u, a, :], words[:, 256 * g + u : 256 * (g + 1) : 2], ident[:]
+                        )
+                pair_banks[q].append(b)
+
+        def copy_pair(q, engs="sss"):
+            gr = work.tile([P, KT, 1024], BF16, name="pairg", tag="pairg", bufs=2, align_bytes=64)
+            for g in range(KT):
+                copy(
+                    engs[g],
+                    gr[:, g, :].bitcast(F32).rearrange("p (r u) -> p r u", u=2),
+                    pair_banks[q][g][:].rearrange("p (u r) -> p r u", u=2),
+                )
+            pair_grouped[q] = gr
+
+        def quantize_pair(q):
+            pair_q[q] = operand("pairq", KT * 256, 3) if q < 6 else operand("compq%d" % q, KT * 256)
+            for g in range(KT):
+                quantize(pair_q[q], 256 * g, 256, pair_grouped[q][:, g, :])
+
+        ys, h1s, h1rs, h1gs, h1q, accs, ht = {}, {}, {}, {}, {}, {}, {}
+        zs, h2g, h2q, s2b = {}, {}, {}, {}
+
+        def make_y(i):
+            ys[i] = work.tile([P, L], F32, name="y", tag="y", bufs=2)
+            g, j = i // 4, i % 4
+            nc.scalar.activation(
+                out=ys[i][:], in_=light_raw[g][:, j, :], func=ACT.Copy, scale=cg[:, g, j : j + 1]
+            )
+
+        def stage1(i):
+            for h in range(2):
+                b = bank("acc%d" % h)
+                for g in range(KT):
+                    mm(b[:], pair_q[i // 2], 256 * g + P * (i % 2), light_q[g], H * h, H, g == 0, g == KT - 1)
+                accs[i, h] = b
+
+        def make_h1(i):
+            h1s[i] = work.tile([P, L], F32, name="h1", tag="h1", bufs=2)
+            for h in range(2):
+                c = slice(H * h, H * (h + 1))
+                nc.vector.scalar_tensor_tensor(
+                    out=h1s[i][:, c], in0=accs[i, h][:], scalar=0.0, in1=ys[i][:, c], op0=ALU.max, op1=ALU.subtract
+                )
+
+        def round_h1(i):
+            h1rs[i] = work.tile([P, L], BF16, name="h1r", tag="h1r", bufs=2, align_bytes=64)
+            copy(
+                "s",
+                h1rs[i][:].rearrange("p (u w e) -> p u w e", u=2, e=2),
+                h1s[i][:].rearrange("p (w u e) -> p u w e", u=2, e=2),
+            )
+
+        def turn_h1(i):
+            b = bank("ht")
+            words = h1rs[i][:].bitcast(F32)
+            for c in range(4):
+                nc.tensor.transpose(b[:, P * c : P * (c + 1)], words[:, P * c : P * (c + 1)], ident[:])
+            ht[i] = b
+
+        def copy_h1(i):
+            h1gs[i] = work.tile([P, 1024], BF16, name="h1g", tag="h1g", bufs=2, align_bytes=64)
+            copy(
+                "s",
+                h1gs[i][:].bitcast(F32).rearrange("p (r u) -> p r u", u=2),
+                ht[i][:].rearrange("p (u r) -> p r u", u=2),
+            )
+
+        def quantize_h1(i):
+            h1q[i] = operand("h1q", 256, 8)
+            quantize(h1q[i], 0, 256, h1gs[i][:])
+
+        def make_z(i):
+            g, j = i // 4, i % 4
+            if j == 0:
+                zs[g] = work.tile([P, 4, L], F32, name="z", tag="z", bufs=2)
+            nc.vector.tensor_tensor(out=zs[g][:, j, :], in0=h1s[i][:], in1=lg_b[:], op=ALU.mult)
+
+        def stage2(g, c):
+            b = bank("s2%d" % (c % 2))
+            for j in range(4):
+                for k in range(KL):
+                    mm(b[:, P * j : P * (j + 1)], h1q[4 * g + j], P * k, transfer_q[k], P * c, P, k == 0, k == KL - 1)
+            s2b[g, c] = b
+
+        def make_h2(g, c):
+            h, o = c // 4, P * (c % 4)
+            if c % 4 == 0:
+                h2g[g, h] = work.tile([P, H, 4], BF16, name="h2g", tag="h2g", bufs=2, align_bytes=64)
+            nc.vector.tensor_tensor(
+                out=h2g[g, h][:, o : o + P, :].rearrange("p (c i) t -> p c t i", i=4),
+                in0=s2b[g, c][:].rearrange("p (t c i) -> p c t i", t=4, i=4),
+                in1=zs[g][:, :, P * c : P * (c + 1)].rearrange("p t (c i) -> p c t i", i=4),
+                op=ALU.add,
+            )
+
+        def quantize_h2(g, h):
+            h2q[g, h] = operand("h2q%d%d" % (g, h), H)
+            quantize(h2q[g, h], 0, H, h2g[g, h][:].rearrange("p n t -> p (n t)"))
+
+        s3 = {}
+
+        def stage3(m, h, gs, tag=None):
+            if tag is not None:
+                s3[m, h] = bank(tag)
+            for g in gs:
+                mm(s3[m, h][:], pair_q[6 + m // 2], 256 * g + P * (m % 2), h2q[g, h], 0, H, g == 0, g == KT - 1)
+
+        out_rows = out.rearrange("(p m) l -> p m l", m=4)
+
+        def store(m, h, eng):
+            r = work.tile([P, H], F32, name="res", tag="res", bufs=4)
+            if eng == "s":
+                nc.scalar.activation(
+                    out=r[:], in_=s3[m, h][:], func=ACT.Identity, scale=-1.0, bias=bias_f[:, m : m + 1]
+                )
+            else:
+                nc.vector.tensor_scalar(
+                    out=r[:], in0=s3[m, h][:], scalar1=bias_f[:, m : m + 1], scalar2=-1.0, op0=ALU.subtract, op1=ALU.mult
+                )
+            nc.sync.dma_start(out=out_rows[:, m, H * h : H * (h + 1)], in_=r[:])
+
+        gr = {}
+        gr[0, 0] = interleave("v", light_raw[0], 0)
+        gr[0, 1] = interleave("s", light_raw[0], 1)
+        quantize(light_q[0], 0, H, gr[0, 0][:].rearrange("p n t -> p (n t)"))
+        gr[1, 0] = interleave("v", light_raw[1], 0)
+        gr[1, 1] = interleave("s", light_raw[1], 1)
+        quantize(light_q[0], H, H, gr[0, 1][:].rearrange("p n t -> p (n t)"))
+        turn_pair(0)
+        quantize(light_q[1], 0, H, gr[1, 0][:].rearrange("p n t -> p (n t)"))
+        copy_pair(0)
+        gr[2, 0] = interleave("v", light_raw[2], 0)
+        quantize(light_q[1], H, H, gr[1, 1][:].rearrange("p n t -> p (n t)"))
+        gr[2, 1] = interleave("s", light_raw[2], 1)
+        quantize(light_q[2], 0, H, gr[2, 0][:].rearrange("p n t -> p (n t)"))
+        quantize_pair(0)
+        quantize(light_q[2], H, H, gr[2, 1][:].rearrange("p n t -> p (n t)"))
+        make_y(0)
+
+        tr_eng = "vvsv"
+        tr = {}
+        bias_f = keep.tile([P, 4], F32, name="bias_f", tag="bias_f")
+        for i in range(NT):
+            g = (i - 4) // 4
+            stage1(i)
+            if i >= 5:
+                gp, cp = (i - 5) // 4, 2 * ((i - 5) % 4)
+                make_h2(gp, cp)
+            if i >= 1:
+                make_z(i - 1)
+            if i >= 5:
+                make_h2(gp, cp + 1)
+            if i < 4:
+                tr[i] = interleave(tr_eng[i], transfer_raw[i // 2], i % 2)
+            make_h1(i)
+            if i + 1 < NT:
+                make_y(i + 1)
+            if i >= 1:
+                turn_h1(i - 1)
+            if i % 2 == 0:
+                turn_pair(i // 2 + 1)
+            elif i == NT - 1:
+                turn_pair(7)
+            if i >= 1:
+                copy_h1(i - 1)
+            if i % 2 == 0:
+                copy_pair(i // 2 + 1)
+            elif i == NT - 1:
+                quantize_pair(6)
+                copy_pair(7)
+            if i >= 1:
+                quantize_h1(i - 1)
+            if i % 2 == 1 and i < NT - 1:
+                quantize_pair((i + 1) // 2)
+            if i < 4:
+                quantize(transfer_q[i // 2], H * (i % 2), H, tr[i][:].rearrange("p n t -> p (n t)"))
+            round_h1(i)
+            if i >= 4:
+                stage2(g, 2 * (i % 4))
+                stage2(g, 2 * (i % 4) + 1)
+            if i >= 5 and cp % 4 == 2:
+                quantize_h2(gp, cp // 4)
+
+        quantize_pair(7)
+        make_h2(1, 6)
+        make_z(NT - 1)
+        make_h2(1, 7)
+        nc.vector.tensor_copy(out=bias_f[:], in_=bias_b[:])
+        for m, tag in enumerate(("acc0", "acc1", "st0", "st1")):
+            stage3(m, 0, (0, 1), tag)
+        turn_h1(NT - 1)
+        copy_h1(NT - 1)
+        quantize_h1(NT - 1)
+        quantize_h2(1, 1)
+        for c in range(8):
+            stage2(2, c)
+            make_h2(2, c)
+            if c == 3:
+                quantize_h2(2, 0)
+                stage3(0, 1, (0, 1), "st2")
+                stage3(1, 1, (0, 1), "ht")
+            if c == 5:
+                for m in range(4):
+                    stage3(m, 0, (2,))
+                    store(m, 0, "s")
+        quantize_h2(2, 1)
+        for m in range(2):
+            stage3(m, 1, (2,))
+            store(m, 1, "vs"[m])
+        stage3(2, 1, (0, 1, 2), "acc0")
+        store(2, 1, "v")
+        stage3(3, 1, (0, 1, 2), "acc1")
+        store(3, 1, "s")

@@ -21,6 +21,7 @@ KT = T // K
 KL = L // K
 NT = T // P
 H = 512
+ZG = 512
 
 
 def tile_canopy_shading_competition_t1_kernel(
@@ -31,7 +32,6 @@ def tile_canopy_shading_competition_t1_kernel(
         keep = ctx.enter_context(tc.tile_pool(name="keep", bufs=1))
         work = ctx.enter_context(tc.tile_pool(name="work", bufs=2))
         psum = ctx.enter_context(tc.psum_pool(name="psum", bufs=1))
-        ctx.enter_context(tc.manual_schedule())
 
         def load(name, shape, src):
             t = keep.tile(shape, BF16, name=name, tag=name, align_bytes=64)
@@ -178,13 +178,23 @@ def tile_canopy_shading_competition_t1_kernel(
                     mm(b[:], pair_q[i // 2], 256 * g + P * (i % 2), light_q[g], H * h, H, g == 0, g == KT - 1)
                 accs[i, h] = b
 
+        def mul_z(eng, i, lo, hi):
+            g, j = i // 4, i % 4
+            if g not in zs:
+                zs[g] = work.tile([P, 4, L], F32, name="z", tag="z", bufs=2)
+            eng.tensor_tensor(out=zs[g][:, j, lo:hi], in0=h1s[i][:, lo:hi], in1=lg_b[:, lo:hi], op=ALU.mult)
+
         def make_h1(i):
-            h1s[i] = work.tile([P, L], F32, name="h1", tag="h1", bufs=2)
+            h1s[i] = work.tile([P, L], F32, name="h1", tag="h1", bufs=3)
             for h in range(2):
                 c = slice(H * h, H * (h + 1))
                 nc.vector.scalar_tensor_tensor(
                     out=h1s[i][:, c], in0=accs[i, h][:], scalar=0.0, in1=ys[i][:, c], op0=ALU.max, op1=ALU.subtract
                 )
+                if h == 0:
+                    mul_z(nc.gpsimd, i, 0, min(H, ZG))
+                elif ZG > H:
+                    mul_z(nc.gpsimd, i, H, ZG)
 
         def round_h1(i):
             h1rs[i] = work.tile([P, L], BF16, name="h1r", tag="h1r", bufs=2, align_bytes=64)
@@ -214,10 +224,8 @@ def tile_canopy_shading_competition_t1_kernel(
             quantize(h1q[i], 0, 256, h1gs[i][:])
 
         def make_z(i):
-            g, j = i // 4, i % 4
-            if j == 0:
-                zs[g] = work.tile([P, 4, L], F32, name="z", tag="z", bufs=2)
-            nc.vector.tensor_tensor(out=zs[g][:, j, :], in0=h1s[i][:], in1=lg_b[:], op=ALU.mult)
+            if ZG < L:
+                mul_z(nc.vector, i, ZG, L)
 
         def stage2(g, c):
             b = bank("s2%d" % (c % 2))
@@ -263,40 +271,44 @@ def tile_canopy_shading_competition_t1_kernel(
                 )
             nc.sync.dma_start(out=out_rows[:, m, H * h : H * (h + 1)], in_=r[:])
 
+        def q_light(g, h):
+            quantize(light_q[g], H * h, H, gr[g, h][:].rearrange("p n t -> p (n t)"))
+
         gr = {}
         gr[0, 0] = interleave("v", light_raw[0], 0)
         gr[0, 1] = interleave("s", light_raw[0], 1)
-        quantize(light_q[0], 0, H, gr[0, 0][:].rearrange("p n t -> p (n t)"))
         gr[1, 0] = interleave("v", light_raw[1], 0)
+        q_light(0, 0)
         gr[1, 1] = interleave("s", light_raw[1], 1)
-        quantize(light_q[0], H, H, gr[0, 1][:].rearrange("p n t -> p (n t)"))
-        turn_pair(0)
-        quantize(light_q[1], 0, H, gr[1, 0][:].rearrange("p n t -> p (n t)"))
-        copy_pair(0)
+        q_light(0, 1)
         gr[2, 0] = interleave("v", light_raw[2], 0)
-        quantize(light_q[1], H, H, gr[1, 1][:].rearrange("p n t -> p (n t)"))
-        gr[2, 1] = interleave("s", light_raw[2], 1)
-        quantize(light_q[2], 0, H, gr[2, 0][:].rearrange("p n t -> p (n t)"))
+        q_light(1, 0)
+        gr[2, 1] = interleave("v", light_raw[2], 1)
+        q_light(2, 0)
+        turn_pair(0)
+        copy_pair(0)
+        q_light(1, 1)
+        q_light(2, 1)
         quantize_pair(0)
-        quantize(light_q[2], H, H, gr[2, 1][:].rearrange("p n t -> p (n t)"))
         make_y(0)
 
-        tr_eng = "vvsv"
         tr = {}
         bias_f = keep.tile([P, 4], F32, name="bias_f", tag="bias_f")
+        s2_steps = [0, 0, 0, 0, 2, 2, 2, 2, 1, 2, 2, 1]
+        chunks = [(g, c) for g in range(KT) for c in range(8)]
+        done2 = 0
+        doneh = 0
         for i in range(NT):
-            g = (i - 4) // 4
             stage1(i)
-            if i >= 5:
-                gp, cp = (i - 5) // 4, 2 * ((i - 5) % 4)
-                make_h2(gp, cp)
-            if i >= 1:
-                make_z(i - 1)
-            if i >= 5:
-                make_h2(gp, cp + 1)
-            if i < 4:
-                tr[i] = interleave(tr_eng[i], transfer_raw[i // 2], i % 2)
             make_h1(i)
+            for g, c in chunks[doneh:done2]:
+                make_h2(g, c)
+            if i < 4:
+                tr[i] = interleave("vvsv"[i], transfer_raw[i // 2], i % 2)
+            for g, c in chunks[doneh:done2]:
+                if c % 4 == 3:
+                    quantize_h2(g, c // 4)
+            doneh = done2
             if i + 1 < NT:
                 make_y(i + 1)
             if i >= 1:
@@ -307,51 +319,62 @@ def tile_canopy_shading_competition_t1_kernel(
                 turn_pair(7)
             if i >= 1:
                 copy_h1(i - 1)
+                make_z(i)
+                quantize_h1(i - 1)
+            else:
+                make_z(i)
             if i % 2 == 0:
                 copy_pair(i // 2 + 1)
             elif i == NT - 1:
                 quantize_pair(6)
-                copy_pair(7)
-            if i >= 1:
-                quantize_h1(i - 1)
             if i % 2 == 1 and i < NT - 1:
                 quantize_pair((i + 1) // 2)
             if i < 4:
                 quantize(transfer_q[i // 2], H * (i % 2), H, tr[i][:].rearrange("p n t -> p (n t)"))
             round_h1(i)
-            if i >= 4:
-                stage2(g, 2 * (i % 4))
-                stage2(g, 2 * (i % 4) + 1)
-            if i >= 5 and cp % 4 == 2:
-                quantize_h2(gp, cp // 4)
+            if i == NT - 1:
+                copy_pair(7)
+            for g, c in chunks[done2 : done2 + s2_steps[i]]:
+                stage2(g, c)
+            done2 += s2_steps[i]
 
-        quantize_pair(7)
-        make_h2(1, 6)
-        make_z(NT - 1)
-        make_h2(1, 7)
-        nc.vector.tensor_copy(out=bias_f[:], in_=bias_b[:])
-        for m, tag in enumerate(("acc0", "acc1", "st0", "st1")):
-            stage3(m, 0, (0, 1), tag)
+        for g, c in chunks[doneh:done2]:
+            make_h2(g, c)
+        doneh = done2
+        for g, c in chunks[done2:16]:
+            stage2(g, c)
         turn_h1(NT - 1)
+        for g, c in chunks[done2:16]:
+            make_h2(g, c)
         copy_h1(NT - 1)
         quantize_h1(NT - 1)
+        quantize_pair(7)
         quantize_h2(1, 1)
-        for c in range(8):
-            stage2(2, c)
-            make_h2(2, c)
-            if c == 3:
-                quantize_h2(2, 0)
-                stage3(0, 1, (0, 1), "st2")
-                stage3(1, 1, (0, 1), "ht")
-            if c == 5:
-                for m in range(4):
-                    stage3(m, 0, (2,))
-                    store(m, 0, "s")
+        nc.vector.tensor_copy(out=bias_f[:], in_=bias_b[:])
+        stage2(2, 0)
+        stage2(2, 1)
+        make_h2(2, 0)
+        make_h2(2, 1)
+        for m, tag in enumerate(("acc0", "acc1", "st0", "st1")):
+            stage3(m, 0, (0, 1), tag)
+            if m % 2 == 1:
+                stage2(2, 2 + m // 2)
+                make_h2(2, 2 + m // 2)
+        stage2(2, 4)
+        stage2(2, 5)
+        quantize_h2(2, 0)
+        make_h2(2, 4)
+        make_h2(2, 5)
+        for m in range(4):
+            stage3(m, 0, (2,))
+            store(m, 0, "s")
+        stage2(2, 6)
+        stage2(2, 7)
+        make_h2(2, 6)
+        make_h2(2, 7)
         quantize_h2(2, 1)
-        for m in range(2):
+        for m, tag in enumerate(("st2", "ht", "acc0", "acc1")):
+            stage3(m, 1, (0, 1), tag)
+        for m in range(4):
             stage3(m, 1, (2,))
-            store(m, 1, "vs"[m])
-        stage3(2, 1, (0, 1, 2), "acc0")
-        store(2, 1, "v")
-        stage3(3, 1, (0, 1, 2), "acc1")
-        store(3, 1, "s")
+            store(m, 1, "vs"[m % 2])

from contextlib import ExitStack

import concourse.mybir as mybir
from concourse.masks import make_identity

T, L, S = 1536, 1024, 512

FLOPS = 2 * (T * T * L + T * L * L + S * T * L)

F32 = mybir.dt.float32
BF16 = mybir.dt.bfloat16
U32 = mybir.dt.uint32
U8 = mybir.dt.uint8
FP8X4 = mybir.dt.float8_e4m3fn_x4
ALU = mybir.AluOpType
ACT = mybir.ActivationFunctionType

P = 128
K = 512
KT = T // K
KL = L // K
NT = T // P
H = 512
ZG = 512


def tile_canopy_shading_competition_t1_kernel(
    tc, light, shade, crown_gain, transfer, layer_gain, compete, bias, out
):
    nc = tc.nc
    with ExitStack() as ctx:
        keep = ctx.enter_context(tc.tile_pool(name="keep", bufs=1))
        work = ctx.enter_context(tc.tile_pool(name="work", bufs=2))
        psum = ctx.enter_context(tc.psum_pool(name="psum", bufs=1))

        def load(name, shape, src):
            t = keep.tile(shape, BF16, name=name, tag=name, align_bytes=64)
            nc.sync.dma_start(out=t[:], in_=src)
            return t

        light_rows = [
            light[K * g : K * (g + 1), :].rearrange("(p j) l -> p j l", j=4) for g in range(KT)
        ]
        cg_b = load("cg_b", [P, KT, 4], crown_gain.rearrange("(g p j) -> p g j", g=KT, j=4))
        light_raw = []
        shade_raw = []

        def load_light(g):
            t = keep.tile([P, 4, L], BF16, name="light%d" % g, tag="light%d" % g, align_bytes=64)
            for h in range(2):
                nc.sync.dma_start(
                    out=t[:, :, H * h : H * (h + 1)], in_=light_rows[g][:, :, H * h : H * (h + 1)]
                )
            light_raw.append(t)

        def load_shade(q):
            g, a = q // 2, 2 * (q % 2)
            src = shade[K * g : K * (g + 1), :].rearrange("(p j) k -> p j k", j=4)
            t = work.tile([P, 2, T], BF16, name="rows", tag="rows", bufs=4, align_bytes=64)
            nc.sync.dma_start(out=t[:], in_=src[:, a : a + 2, :])
            shade_raw.append(t)

        load_light(0)
        load_light(1)
        load_shade(0)
        load_light(2)
        load_shade(1)
        transfer_raw = [
            load("transfer%d" % g, [P, 4, L], transfer[K * g : K * (g + 1), :].rearrange("(p j) n -> p j n", j=4))
            for g in range(KL)
        ]
        lg_b = load("lg_b", [P, L], layer_gain.partition_broadcast(P))
        for q in range(2, 6):
            load_shade(q)
        compete_rows = compete.rearrange("(p m) k -> p m k", m=4)
        for q in range(2):
            t = work.tile([P, 2, T], BF16, name="rows", tag="rows", bufs=4, align_bytes=64)
            nc.sync.dma_start(out=t[:], in_=compete_rows[:, 2 * q : 2 * q + 2, :])
            shade_raw.append(t)
        bias_b = load("bias_b", [P, 4], bias.rearrange("(p m) -> p m", m=4))

        ident = keep.tile([P, P], F32, name="ident", tag="ident")
        make_identity(nc, ident[:])
        warm = keep.tile([P, 1], F32, name="warm", tag="warm")
        nc.vector.memset(warm[:], 0.0)
        nc.scalar.activation(out=warm[:], in_=warm[:], func=ACT.Copy)
        cg = keep.tile([P, KT, 4], F32, name="cg", tag="cg")
        nc.vector.tensor_copy(out=cg[:], in_=cg_b[:])

        def operand(name, cols, bufs=1):
            codes = keep.tile([P, cols], U32, name=name + "_c", tag=name + "_c", bufs=bufs, align_bytes=64)
            scales = keep.tile([P, cols], U8, name=name + "_s", tag=name + "_s", bufs=bufs, align_bytes=64)
            return codes, scales

        def quantize(dst, lo, n, grouped):
            nc.vector.quantize_mx(
                out=dst[0][:, lo : lo + n].bitcast(FP8X4), scales=dst[1][:, lo : lo + n], in_=grouped
            )

        def mm(acc, st, so, mv, mo, n, start, stop):
            nc.tensor.matmul_mx(
                out=acc,
                lhsT=st[0][:, so : so + P].bitcast(FP8X4),
                lhsT_scale=st[1][:, so : so + P],
                rhs=mv[0][:, mo : mo + n].bitcast(FP8X4),
                rhs_scale=mv[1][:, mo : mo + n],
                start=start,
                stop=stop,
            )

        def copy(eng, dst, src):
            if eng == "v":
                nc.vector.tensor_copy(out=dst, in_=src)
            else:
                nc.scalar.copy(out=dst, in_=src)

        def bank(tag):
            return psum.tile([P, 512], F32, name=tag, tag=tag)

        def interleave(eng, raw, h):
            g = work.tile([P, H, 4], BF16, name="grouped", tag="grouped", bufs=3, align_bytes=64)
            copy(
                eng,
                g[:].rearrange("p (c i) t -> p c t i", i=4),
                raw[:, :, H * h : H * (h + 1)].rearrange("p t (c i) -> p c t i", i=4),
            )
            return g

        light_q = [operand("lightq%d" % g, L) for g in range(KT)]
        transfer_q = [operand("transferq%d" % g, L) for g in range(KL)]

        pair_q = {}
        pair_banks = {}
        pair_grouped = {}

        def turn_pair(q):
            pair_banks[q] = []
            for g in range(KT):
                b = bank("st%d" % g)
                v = b[:].rearrange("p (u a r) -> p u a r", u=2, a=2)
                for a in range(2):
                    words = shade_raw[q][:, a, :].bitcast(F32)
                    for u in range(2):
                        nc.tensor.transpose(
                            v[:, u, a, :], words[:, 256 * g + u : 256 * (g + 1) : 2], ident[:]
                        )
                pair_banks[q].append(b)

        def copy_pair(q, engs="sss"):
            gr = work.tile([P, KT, 1024], BF16, name="pairg", tag="pairg", bufs=2, align_bytes=64)
            for g in range(KT):
                copy(
                    engs[g],
                    gr[:, g, :].bitcast(F32).rearrange("p (r u) -> p r u", u=2),
                    pair_banks[q][g][:].rearrange("p (u r) -> p r u", u=2),
                )
            pair_grouped[q] = gr

        def quantize_pair(q):
            pair_q[q] = operand("pairq", KT * 256, 3) if q < 6 else operand("compq%d" % q, KT * 256)
            for g in range(KT):
                quantize(pair_q[q], 256 * g, 256, pair_grouped[q][:, g, :])

        ys, h1s, h1rs, h1gs, h1q, accs, ht = {}, {}, {}, {}, {}, {}, {}
        zs, h2g, h2q, s2b = {}, {}, {}, {}

        def make_y(i):
            ys[i] = work.tile([P, L], F32, name="y", tag="y", bufs=2)
            g, j = i // 4, i % 4
            nc.scalar.activation(
                out=ys[i][:], in_=light_raw[g][:, j, :], func=ACT.Copy, scale=cg[:, g, j : j + 1]
            )

        def stage1(i):
            for h in range(2):
                b = bank("acc%d" % h)
                for g in range(KT):
                    mm(b[:], pair_q[i // 2], 256 * g + P * (i % 2), light_q[g], H * h, H, g == 0, g == KT - 1)
                accs[i, h] = b

        def mul_z(eng, i, lo, hi):
            g, j = i // 4, i % 4
            if g not in zs:
                zs[g] = work.tile([P, 4, L], F32, name="z", tag="z", bufs=2)
            eng.tensor_tensor(out=zs[g][:, j, lo:hi], in0=h1s[i][:, lo:hi], in1=lg_b[:, lo:hi], op=ALU.mult)

        def make_h1(i):
            h1s[i] = work.tile([P, L], F32, name="h1", tag="h1", bufs=3)
            for h in range(2):
                c = slice(H * h, H * (h + 1))
                nc.vector.scalar_tensor_tensor(
                    out=h1s[i][:, c], in0=accs[i, h][:], scalar=0.0, in1=ys[i][:, c], op0=ALU.max, op1=ALU.subtract
                )
                if h == 0:
                    mul_z(nc.gpsimd, i, 0, min(H, ZG))
                elif ZG > H:
                    mul_z(nc.gpsimd, i, H, ZG)

        def round_h1(i):
            h1rs[i] = work.tile([P, L], BF16, name="h1r", tag="h1r", bufs=2, align_bytes=64)
            copy(
                "s",
                h1rs[i][:].rearrange("p (u w e) -> p u w e", u=2, e=2),
                h1s[i][:].rearrange("p (w u e) -> p u w e", u=2, e=2),
            )

        def turn_h1(i):
            b = bank("ht")
            words = h1rs[i][:].bitcast(F32)
            for c in range(4):
                nc.tensor.transpose(b[:, P * c : P * (c + 1)], words[:, P * c : P * (c + 1)], ident[:])
            ht[i] = b

        def copy_h1(i):
            h1gs[i] = work.tile([P, 1024], BF16, name="h1g", tag="h1g", bufs=2, align_bytes=64)
            copy(
                "s",
                h1gs[i][:].bitcast(F32).rearrange("p (r u) -> p r u", u=2),
                ht[i][:].rearrange("p (u r) -> p r u", u=2),
            )

        def quantize_h1(i):
            h1q[i] = operand("h1q", 256, 8)
            quantize(h1q[i], 0, 256, h1gs[i][:])

        def make_z(i):
            if ZG < L:
                mul_z(nc.vector, i, ZG, L)

        def stage2(g, c):
            b = bank("s2%d" % (c % 2))
            for j in range(4):
                for k in range(KL):
                    mm(b[:, P * j : P * (j + 1)], h1q[4 * g + j], P * k, transfer_q[k], P * c, P, k == 0, k == KL - 1)
            s2b[g, c] = b

        def make_h2(g, c):
            h, o = c // 4, P * (c % 4)
            if c % 4 == 0:
                h2g[g, h] = work.tile([P, H, 4], BF16, name="h2g", tag="h2g", bufs=2, align_bytes=64)
            nc.vector.tensor_tensor(
                out=h2g[g, h][:, o : o + P, :].rearrange("p (c i) t -> p c t i", i=4),
                in0=s2b[g, c][:].rearrange("p (t c i) -> p c t i", t=4, i=4),
                in1=zs[g][:, :, P * c : P * (c + 1)].rearrange("p t (c i) -> p c t i", i=4),
                op=ALU.add,
            )

        def quantize_h2(g, h):
            h2q[g, h] = operand("h2q%d%d" % (g, h), H)
            quantize(h2q[g, h], 0, H, h2g[g, h][:].rearrange("p n t -> p (n t)"))

        s3 = {}

        def stage3(m, h, gs, tag=None):
            if tag is not None:
                s3[m, h] = bank(tag)
            for g in gs:
                mm(s3[m, h][:], pair_q[6 + m // 2], 256 * g + P * (m % 2), h2q[g, h], 0, H, g == 0, g == KT - 1)

        out_rows = out.rearrange("(p m) l -> p m l", m=4)

        def store(m, h, eng):
            r = work.tile([P, H], F32, name="res", tag="res", bufs=4)
            if eng == "s":
                nc.scalar.activation(
                    out=r[:], in_=s3[m, h][:], func=ACT.Identity, scale=-1.0, bias=bias_f[:, m : m + 1]
                )
            else:
                nc.vector.tensor_scalar(
                    out=r[:], in0=s3[m, h][:], scalar1=bias_f[:, m : m + 1], scalar2=-1.0, op0=ALU.subtract, op1=ALU.mult
                )
            nc.sync.dma_start(out=out_rows[:, m, H * h : H * (h + 1)], in_=r[:])

        def q_light(g, h):
            quantize(light_q[g], H * h, H, gr[g, h][:].rearrange("p n t -> p (n t)"))

        gr = {}
        gr[0, 0] = interleave("v", light_raw[0], 0)
        gr[0, 1] = interleave("s", light_raw[0], 1)
        gr[1, 0] = interleave("v", light_raw[1], 0)
        q_light(0, 0)
        gr[1, 1] = interleave("s", light_raw[1], 1)
        q_light(0, 1)
        gr[2, 0] = interleave("v", light_raw[2], 0)
        q_light(1, 0)
        gr[2, 1] = interleave("v", light_raw[2], 1)
        q_light(2, 0)
        turn_pair(0)
        copy_pair(0)
        q_light(1, 1)
        q_light(2, 1)
        quantize_pair(0)
        make_y(0)

        tr = {}
        bias_f = keep.tile([P, 4], F32, name="bias_f", tag="bias_f")
        s2_steps = [0, 0, 0, 0, 2, 2, 2, 2, 1, 2, 2, 1]
        chunks = [(g, c) for g in range(KT) for c in range(8)]
        done2 = 0
        doneh = 0
        for i in range(NT):
            stage1(i)
            make_h1(i)
            for g, c in chunks[doneh:done2]:
                make_h2(g, c)
            if i < 4:
                tr[i] = interleave("vvsv"[i], transfer_raw[i // 2], i % 2)
            for g, c in chunks[doneh:done2]:
                if c % 4 == 3:
                    quantize_h2(g, c // 4)
            doneh = done2
            if i + 1 < NT:
                make_y(i + 1)
            if i >= 1:
                turn_h1(i - 1)
            if i % 2 == 0:
                turn_pair(i // 2 + 1)
            elif i == NT - 1:
                turn_pair(7)
            if i >= 1:
                copy_h1(i - 1)
                make_z(i)
                quantize_h1(i - 1)
            else:
                make_z(i)
            if i % 2 == 0:
                copy_pair(i // 2 + 1)
            elif i == NT - 1:
                quantize_pair(6)
            if i % 2 == 1 and i < NT - 1:
                quantize_pair((i + 1) // 2)
            if i < 4:
                quantize(transfer_q[i // 2], H * (i % 2), H, tr[i][:].rearrange("p n t -> p (n t)"))
            round_h1(i)
            if i == NT - 1:
                copy_pair(7)
            for g, c in chunks[done2 : done2 + s2_steps[i]]:
                stage2(g, c)
            done2 += s2_steps[i]

        for g, c in chunks[doneh:done2]:
            make_h2(g, c)
        doneh = done2
        for g, c in chunks[done2:16]:
            stage2(g, c)
        turn_h1(NT - 1)
        for g, c in chunks[done2:16]:
            make_h2(g, c)
        copy_h1(NT - 1)
        quantize_h1(NT - 1)
        quantize_pair(7)
        quantize_h2(1, 1)
        nc.vector.tensor_copy(out=bias_f[:], in_=bias_b[:])
        stage2(2, 0)
        stage2(2, 1)
        make_h2(2, 0)
        make_h2(2, 1)
        for m, tag in enumerate(("acc0", "acc1", "st0", "st1")):
            stage3(m, 0, (0, 1), tag)
            if m % 2 == 1:
                stage2(2, 2 + m // 2)
                make_h2(2, 2 + m // 2)
        stage2(2, 4)
        stage2(2, 5)
        quantize_h2(2, 0)
        make_h2(2, 4)
        make_h2(2, 5)
        for m in range(4):
            stage3(m, 0, (2,))
            store(m, 0, "s")
        stage2(2, 6)
        stage2(2, 7)
        make_h2(2, 6)
        make_h2(2, 7)
        quantize_h2(2, 1)
        for m, tag in enumerate(("st2", "ht", "acc0", "acc1")):
            stage3(m, 1, (0, 1), tag)
        for m in range(4):
            stage3(m, 1, (2,))
            store(m, 1, "vs"[m % 2])
